import numpy as np
import ml_dtypes


def mxq(x, axis, fmt="e4m3"):
    dtype, down = {"e4m3": (ml_dtypes.float8_e4m3fn, 7), "e5m2": (ml_dtypes.float8_e5m2, 14)}[fmt]
    v = np.moveaxis(np.asarray(x, np.float32).astype(ml_dtypes.bfloat16).astype(np.float64), axis, -1)
    blocks = v.reshape(v.shape[:-1] + (-1, 32))
    amax = np.abs(blocks).max(-1, keepdims=True)
    byte = np.maximum(np.where(amax > 0, np.frexp(amax)[1] - 1 + 127, 0) - down, 1)
    scale = np.exp2(byte - 127.0)
    codes = (blocks / scale).astype(np.float32).astype(dtype).astype(np.float64)
    return np.moveaxis((codes * scale).reshape(v.shape), -1, axis)


WIDE = False


def mx_kscale(k):
    if not WIDE:
        return np.ones(k)
    levels = np.array([10, -10, 5, -5, 0])
    if k % 512:
        return np.exp2(np.random.permutation(np.resize(levels, k // 32))).repeat(32)
    a = np.empty((k // 512, 16))
    for p in range(k // 512):
        a[p, :8] = np.random.permutation(np.resize(levels, 8))
        for g in range(8):
            far = levels[np.abs(levels - a[p, g]) >= 10]
            a[p, g + 8] = far[np.random.randint(len(far))]
    return np.exp2(a.ravel()).repeat(32)


def f64(x):
    return np.asarray(x).astype(np.float64)


def striped8(idx):
    return np.concatenate([v.reshape(-1, 16).T for v in idx]).astype(np.uint16)


def unstriped8(offs):
    return np.stack([offs[16 * g:16 * g + 16].T.reshape(-1) for g in range(8)]).astype(np.int64)


def gelu(v):
    return 0.5 * v * (1.0 + np.tanh(np.sqrt(2.0 / np.pi) * (v + 0.044715 * v**3)))


K, M, T, S = 1024, 256, 4096, 2048


def setup_inputs():
    n = np.random.standard_normal
    s = mx_kscale(K)[:, None]
    return {
        "x": (n((K, S)) * s).astype(np.float32),
        "w": (n((K, M)) / np.sqrt(K) / s).astype(np.float32),
        "b": (0.3 * n(256)).astype(np.float32),
        "wgo": np.repeat(np.random.uniform(0.5, 2.0, (8, S)), 16, axis=0).astype(np.float32),
        "offs": striped8(np.stack([np.random.permutation(T)[:S] for _ in range(8)])),
    }


def reference(x, w, b, wgo, offs):
    x_ = mxq(f64(x), 0, "e4m3")
    w_ = mxq(f64(w), 0, "e4m3")
    y = w_.T @ x_
    place = unstriped8(offs)[np.arange(M) % 128 // 16]
    out = np.zeros((M, T))
    out[np.arange(M)[:, None], place] = f64(wgo)[np.arange(M) % 128] * (gelu(y + f64(b)[:, None]))
    return out

@@ -1,0 +1,205 @@
+from contextlib import ExitStack
+
+import concourse.mybir as mybir
+from concourse.masks import make_identity
+
+K, M, T, S = 1024, 256, 4096, 2048
+FLOPS = 2 * K * M * S
+
+F32 = mybir.dt.float32
+BF16 = mybir.dt.bfloat16
+U32 = mybir.dt.uint32
+U16 = mybir.dt.uint16
+U8 = mybir.dt.uint8
+FP8X4 = mybir.dt.float8_e4m3fn_x4
+GELU = mybir.ActivationFunctionType.Gelu_apprx_tanh
+MULT = mybir.AluOpType.mult
+
+P = 128
+PACK = 4
+K_PASS = P * PACK
+PASSES = K // K_PASS
+ROW_TILES = M // P
+HALF = S // 2
+HALVES = S // HALF
+LIST_COLUMNS = HALF // 16
+BANK = 512
+
+LOADS = [
+    [(0, 0, 1024), (1, 0, 512), (1, 512, 384), (1, 896, 128)],
+    [(0, 1024, 512), (1, 1024, 512), (0, 1536, 512), (1, 1536, 512)],
+]
+BLOCKS = [
+    [(0, 512), (512, 256), (768, 128), (896, 128)],
+    [(0, 512), (512, 256), (768, 128), (896, 128)],
+]
+
+
+def interleave(copy, grouped, raw, c0, c1):
+    copy(
+        out=grouped[:, c0:c1, :].rearrange("p (c i) j -> p c j i", i=4),
+        in_=raw[:, :, c0:c1].rearrange("p j (c i) -> p c j i", i=4),
+    )
+
+
+def tile_list_hscat_gelu_kernel(tc, x, w, b, wgo, offs, out):
+    nc = tc.nc
+    with ExitStack() as ctx:
+        keep = ctx.enter_context(tc.tile_pool(name="keep", bufs=1))
+        psum = ctx.enter_context(tc.psum_pool(name="psum", bufs=1))
+
+        offsets = keep.tile([P, S // 16], U16, name="offsets")
+
+        zero = keep.tile([P, 1], F32, name="zero")
+        nc.gpsimd.memset(zero[:], 0.0)
+        table_loaded = keep.tile([P, 1], F32, name="table_loaded")
+        nc.scalar.activation(out=table_loaded[:], in_=zero[:], func=GELU)
+
+        identity = keep.tile([P, P], F32, name="identity")
+        make_identity(nc, identity[:])
+        b_rows = keep.tile([P, P], F32, name="b_rows")
+        nc.gpsimd.memset(b_rows[:], 0.0)
+        nc.scalar.dma_start(out=b_rows[0:ROW_TILES, :], in_=b.rearrange("(m p) -> m p", p=P))
+        b_turned = psum.tile([P, P], F32, name="b_turned")
+        nc.tensor.transpose(b_turned[:], b_rows[:], identity[:])
+
+        w_raw = keep.tile([P, PASSES, PACK, M], F32, name="w_raw")
+        nc.sync.dma_start(
+            out=w_raw[:].rearrange("p a i n -> p a (i n)"),
+            in_=w.rearrange("(a p i) n -> p a (i n)", a=PASSES, i=PACK),
+        )
+        raws = {}
+        factors = []
+        for h in range(HALVES):
+            for load in LOADS[h]:
+                a, c0, width = load
+                if load == LOADS[h][-1]:
+                    tag = f"last_{h}"
+                elif load == LOADS[0][-2]:
+                    tag = "last_but_one"
+                else:
+                    tag = f"raw_{a}_{c0}"
+                raw = keep.tile([P, PACK, width], F32, name=f"raw_{a}_{c0}", tag=tag)
+                nc.sync.dma_start(
+                    out=raw[:],
+                    in_=x[a * K_PASS : (a + 1) * K_PASS, c0 : c0 + width].rearrange("(p i) c -> p i c", i=PACK),
+                )
+                raws[load] = raw
+            if h == 0:
+                nc.sync.dma_start(out=offsets[:], in_=offs)
+            factor = keep.tile([P, HALF], F32, name=f"factor_{h}")
+            if h == 0:
+                nc.sync.dma_start(out=factor[:], in_=wgo[:, 0:HALF])
+            else:
+                nc.sync.dma_start(out=factor[:], in_=wgo[:, HALF:S])
+            factors.append(factor)
+
+        placed = [keep.tile([P, T], F32, name=f"placed_{m}") for m in range(ROW_TILES)]
+        nc.vector.memset(placed[0][:], 0.0)
+        nc.gpsimd.memset(placed[1][:], 0.0)
+
+        w_grouped = keep.tile([P, PASSES, M, PACK], BF16, name="w_grouped", align_bytes=64)
+        for a in range(PASSES):
+            interleave(nc.scalar.copy, w_grouped[:, a, :, :], w_raw[:, a, :, :], 0, M)
+        w_codes = keep.tile([P, PASSES * M], U32, name="w_codes", align_bytes=64)
+        w_scales = keep.tile([P, PASSES * M], U8, name="w_scales", align_bytes=64)
+        nc.vector.quantize_mx(
+            out=w_codes[:].bitcast(FP8X4),
+            scales=w_scales[:],
+            in_=w_grouped[:].rearrange("p a n i -> p (a n i)"),
+        )
+
+        x_codes = [keep.tile([P, S], U32, name=f"x_codes_{a}", align_bytes=64) for a in range(PASSES)]
+        x_scales = [keep.tile([P, S], U8, name=f"x_scales_{a}", align_bytes=64) for a in range(PASSES)]
+        grouped = {}
+        for h in range(HALVES):
+            for load in LOADS[h]:
+                a, c0, width = load
+                grouped[load] = keep.tile([P, width, PACK], BF16, name=f"grouped_{a}_{c0}", align_bytes=64)
+
+        def copy_in(load, c0, c1, vector_columns):
+            split = c0 + vector_columns
+            if vector_columns > 0:
+                interleave(nc.vector.tensor_copy, grouped[load], raws[load], c0, split)
+            interleave(nc.scalar.copy, grouped[load], raws[load], split, c1)
+
+        def quantize(load, c0, c1):
+            a, first, width = load
+            nc.vector.quantize_mx(
+                out=x_codes[a][:, first + c0 : first + c1].bitcast(FP8X4),
+                scales=x_scales[a][:, first + c0 : first + c1],
+                in_=grouped[load][:, c0:c1, :].rearrange("p c i -> p (c i)"),
+            )
+
+        bias = keep.tile([P, ROW_TILES], F32, name="bias", tag="last_but_one")
+
+        def multiply(m, sums, results, h, c0, width):
+            for a in range(PASSES):
+                w_cols = slice(a * M + m * P, a * M + (m + 1) * P)
+                x_cols = slice(h * HALF + c0, h * HALF + c0 + width)
+                nc.tensor.matmul_mx(
+                    out=sums,
+                    lhsT=w_codes[:, w_cols].bitcast(FP8X4),
+                    lhsT_scale=w_scales[:, w_cols],
+                    rhs=x_codes[a][:, x_cols].bitcast(FP8X4),
+                    rhs_scale=x_scales[a][:, x_cols],
+                    start=(a == 0),
+                    stop=(a == PASSES - 1),
+                )
+            nc.scalar.activation(out=results[:, c0 : c0 + width], in_=sums, func=GELU, bias=bias[:, m : m + 1])
+
+        def place(m, results, h):
+            nc.vector.tensor_tensor(
+                placed[m][:].indirect(offsets[:, h * LIST_COLUMNS : (h + 1) * LIST_COLUMNS]),
+                results[:],
+                factors[h][:],
+                MULT,
+            )
+
+        def first_row_tile(h):
+            results = keep.tile([P, HALF], F32, name=f"results_0_{h}", tag=f"last_{h}")
+            for block in BLOCKS[h]:
+                c0, width = block
+                if block == BLOCKS[h][-1]:
+                    sums = psum.tile([P, HALF], F32, name=f"sums_0_{h}_last", tag="late")
+                else:
+                    sums = psum.tile([P, BANK], F32, name=f"sums_0_{h}_{c0}", tag=f"sums_{c0}")
+                multiply(0, sums[:, 0:width], results, h, c0, width)
+            return results
+
+        def second_row_tile(h):
+            results = keep.tile([P, HALF], F32, name=f"results_1_{h}")
+            sums = psum.tile([P, HALF], F32, name=f"sums_1_{h}", tag="late")
+            for c0 in range(0, HALF, BANK):
+                multiply(1, sums[:, c0 : c0 + BANK], results, h, c0, BANK)
+            return results
+
+        whole, wide, narrow, last = LOADS[0]
+        copy_in(whole, 0, 512, 320)
+        quantize(whole, 0, 512)
+        copy_in(whole, 512, 1024, 320)
+        quantize(whole, 512, 1024)
+        copy_in(wide, 0, 512, 320)
+        quantize(wide, 0, 512)
+        copy_in(narrow, 0, 384, 224)
+        quantize(narrow, 0, 256)
+        quantize(narrow, 256, 384)
+        nc.scalar.copy(out=bias[:], in_=b_turned[:, 0:ROW_TILES])
+        copy_in(last, 0, 128, 64)
+        quantize(last, 0, 128)
+        place(0, first_row_tile(0), 0)
+        results = second_row_tile(0)
+
+        for load in LOADS[1]:
+            copy_in(load, 0, 512, 0)
+        quantize(LOADS[1][0], 0, 512)
+        place(1, results, 0)
+        quantize(LOADS[1][1], 0, 512)
+        quantize(LOADS[1][2], 0, 512)
+        quantize(LOADS[1][3], 0, 256)
+        quantize(LOADS[1][3], 256, 384)
+        quantize(LOADS[1][3], 384, 512)
+        place(0, first_row_tile(1), 1)
+        nc.sync.dma_start(out=out[0:P, :], in_=placed[0][:])
+        place(1, second_row_tile(1), 1)
+        nc.sync.dma_start(out=out[P:M, :], in_=placed[1][:])

@@ -1,7 +1,6 @@
 from contextlib import ExitStack
 
 import concourse.mybir as mybir
-from concourse.masks import make_identity
 
 K, M, T, S = 1024, 256, 4096, 2048
 FLOPS = 2 * K * M * S
@@ -20,19 +19,27 @@ PACK = 4
 K_PASS = P * PACK
 PASSES = K // K_PASS
 ROW_TILES = M // P
-HALF = S // 2
-HALVES = S // HALF
-LIST_COLUMNS = HALF // 16
 BANK = 512
+LIST_ROWS = 16
 
-LOADS = [
-    [(0, 0, 1024), (1, 0, 512), (1, 512, 384), (1, 896, 128)],
-    [(0, 1024, 512), (1, 1024, 512), (0, 1536, 512), (1, 1536, 512)],
-]
-BLOCKS = [
-    [(0, 512), (512, 256), (768, 128), (896, 128)],
-    [(0, 512), (512, 256), (768, 128), (896, 128)],
-]
+CHUNKS = [256] * 8
+FACTOR_LOADS = {0: 256, 1: 256, 2: 512, 4: 1024}
+LAGGING = [256, 256, 256, 256, 256, 768]
+FIRST_VECTOR_COLUMNS = [128, 160]
+
+
+def starts(widths):
+    return [sum(widths[:i]) for i in range(len(widths))]
+
+
+def powers_of_two(width):
+    pieces = []
+    c0 = 0
+    for piece in (512, 256, 128):
+        while width - c0 >= piece:
+            pieces.append((c0, piece))
+            c0 += piece
+    return pieces
 
 
 def interleave(copy, grouped, raw, c0, c1):
@@ -46,160 +53,120 @@ def tile_list_hscat_gelu_kernel(tc, x, w, b, wgo, offs, out):
     nc = tc.nc
     with ExitStack() as ctx:
         keep = ctx.enter_context(tc.tile_pool(name="keep", bufs=1))
-        psum = ctx.enter_context(tc.psum_pool(name="psum", bufs=1))
+        psum = ctx.enter_context(tc.psum_pool(name="psum", bufs=3))
 
-        offsets = keep.tile([P, S // 16], U16, name="offsets")
+        offsets = keep.tile([P, S // LIST_ROWS], U16, name="offsets")
+
+        bias = keep.tile([P, ROW_TILES], F32, name="bias")
+        with nc.allow_non_contiguous_dma(reason="one bias to a partition"):
+            nc.scalar.dma_start(out=bias[:], in_=b.rearrange("(m p) -> p m", p=P))
 
         zero = keep.tile([P, 1], F32, name="zero")
         nc.gpsimd.memset(zero[:], 0.0)
         table_loaded = keep.tile([P, 1], F32, name="table_loaded")
         nc.scalar.activation(out=table_loaded[:], in_=zero[:], func=GELU)
 
-        identity = keep.tile([P, P], F32, name="identity")
-        make_identity(nc, identity[:])
-        b_rows = keep.tile([P, P], F32, name="b_rows")
-        nc.gpsimd.memset(b_rows[:], 0.0)
-        nc.scalar.dma_start(out=b_rows[0:ROW_TILES, :], in_=b.rearrange("(m p) -> m p", p=P))
-        b_turned = psum.tile([P, P], F32, name="b_turned")
-        nc.tensor.transpose(b_turned[:], b_rows[:], identity[:])
+        first_bias = keep.tile([P, 1], F32, name="first_bias", tag="grouped_1_0", align_bytes=64)
+        nc.scalar.copy(out=first_bias[:], in_=bias[:, 0:1])
 
-        w_raw = keep.tile([P, PASSES, PACK, M], F32, name="w_raw")
-        nc.sync.dma_start(
-            out=w_raw[:].rearrange("p a i n -> p a (i n)"),
-            in_=w.rearrange("(a p i) n -> p a (i n)", a=PASSES, i=PACK),
-        )
+        w_raw = []
         raws = {}
-        factors = []
-        for h in range(HALVES):
-            for load in LOADS[h]:
-                a, c0, width = load
-                if load == LOADS[h][-1]:
-                    tag = f"last_{h}"
-                elif load == LOADS[0][-2]:
-                    tag = "last_but_one"
-                else:
-                    tag = f"raw_{a}_{c0}"
-                raw = keep.tile([P, PACK, width], F32, name=f"raw_{a}_{c0}", tag=tag)
+        factor = keep.tile([P, S], F32, name="factor")
+        for c, (c0, width) in enumerate(zip(starts(CHUNKS), CHUNKS)):
+            for a in range(PASSES):
+                if c == 0:
+                    rows = keep.tile([P, PACK, M], F32, name=f"w_raw_{a}")
+                    nc.sync.dma_start(
+                        out=rows[:].rearrange("p i n -> p (i n)"),
+                        in_=w[a * K_PASS : (a + 1) * K_PASS, :].rearrange("(p i) n -> p (i n)", i=PACK),
+                    )
+                    w_raw.append(rows)
+            for a in range(PASSES):
+                raw = keep.tile([P, PACK, width], F32, name=f"raw_{c}_{a}", tag=f"raw_{c}_{a}")
                 nc.sync.dma_start(
                     out=raw[:],
                     in_=x[a * K_PASS : (a + 1) * K_PASS, c0 : c0 + width].rearrange("(p i) c -> p i c", i=PACK),
                 )
-                raws[load] = raw
-            if h == 0:
+                raws[c, a] = raw
+            if c == 0:
                 nc.sync.dma_start(out=offsets[:], in_=offs)
-            factor = keep.tile([P, HALF], F32, name=f"factor_{h}")
-            if h == 0:
-                nc.sync.dma_start(out=factor[:], in_=wgo[:, 0:HALF])
-            else:
-                nc.sync.dma_start(out=factor[:], in_=wgo[:, HALF:S])
-            factors.append(factor)
+            if c in FACTOR_LOADS:
+                f0 = sum(run for chunk, run in FACTOR_LOADS.items() if chunk < c)
+                f1 = f0 + FACTOR_LOADS[c]
+                nc.sync.dma_start(out=factor[:, f0:f1], in_=wgo[:, f0:f1])
 
         placed = [keep.tile([P, T], F32, name=f"placed_{m}") for m in range(ROW_TILES)]
-        nc.vector.memset(placed[0][:], 0.0)
+        nc.vector.memset(placed[0][:, 0 : T // 2 - 1], 0.0)
+        nc.vector.memset(placed[0][:, T // 2 - 1 : T], 0.0)
         nc.gpsimd.memset(placed[1][:], 0.0)
 
-        w_grouped = keep.tile([P, PASSES, M, PACK], BF16, name="w_grouped", align_bytes=64)
-        for a in range(PASSES):
-            interleave(nc.scalar.copy, w_grouped[:, a, :, :], w_raw[:, a, :, :], 0, M)
         w_codes = keep.tile([P, PASSES * M], U32, name="w_codes", align_bytes=64)
         w_scales = keep.tile([P, PASSES * M], U8, name="w_scales", align_bytes=64)
-        nc.vector.quantize_mx(
-            out=w_codes[:].bitcast(FP8X4),
-            scales=w_scales[:],
-            in_=w_grouped[:].rearrange("p a n i -> p (a n i)"),
-        )
+        for a in range(PASSES):
+            w_grouped = keep.tile([P, M, PACK], BF16, name=f"w_grouped_{a}", align_bytes=64)
+            interleave(nc.scalar.copy, w_grouped, w_raw[a], 0, M)
+            nc.vector.quantize_mx(
+                out=w_codes[:, a * M : (a + 1) * M].bitcast(FP8X4),
+                scales=w_scales[:, a * M : (a + 1) * M],
+                in_=w_grouped[:].rearrange("p n i -> p (n i)"),
+            )
 
         x_codes = [keep.tile([P, S], U32, name=f"x_codes_{a}", align_bytes=64) for a in range(PASSES)]
         x_scales = [keep.tile([P, S], U8, name=f"x_scales_{a}", align_bytes=64) for a in range(PASSES)]
-        grouped = {}
-        for h in range(HALVES):
-            for load in LOADS[h]:
-                a, c0, width = load
-                grouped[load] = keep.tile([P, width, PACK], BF16, name=f"grouped_{a}_{c0}", align_bytes=64)
 
-        def copy_in(load, c0, c1, vector_columns):
-            split = c0 + vector_columns
-            if vector_columns > 0:
-                interleave(nc.vector.tensor_copy, grouped[load], raws[load], c0, split)
-            interleave(nc.scalar.copy, grouped[load], raws[load], split, c1)
-
-        def quantize(load, c0, c1):
-            a, first, width = load
-            nc.vector.quantize_mx(
-                out=x_codes[a][:, first + c0 : first + c1].bitcast(FP8X4),
-                scales=x_scales[a][:, first + c0 : first + c1],
-                in_=grouped[load][:, c0:c1, :].rearrange("p c i -> p (c i)"),
-            )
-
-        bias = keep.tile([P, ROW_TILES], F32, name="bias", tag="last_but_one")
-
-        def multiply(m, sums, results, h, c0, width):
-            for a in range(PASSES):
-                w_cols = slice(a * M + m * P, a * M + (m + 1) * P)
-                x_cols = slice(h * HALF + c0, h * HALF + c0 + width)
-                nc.tensor.matmul_mx(
-                    out=sums,
-                    lhsT=w_codes[:, w_cols].bitcast(FP8X4),
-                    lhsT_scale=w_scales[:, w_cols],
-                    rhs=x_codes[a][:, x_cols].bitcast(FP8X4),
-                    rhs_scale=x_scales[a][:, x_cols],
-                    start=(a == 0),
-                    stop=(a == PASSES - 1),
+        def prepare(c, a):
+            first, width = starts(CHUNKS)[c], CHUNKS[c]
+            grouped = keep.tile([P, width, PACK], BF16, name=f"grouped_{c}_{a}", tag=f"grouped_{c}_{a}", align_bytes=64)
+            split = FIRST_VECTOR_COLUMNS[a] if c == 0 else 0
+            if split > 0:
+                interleave(nc.vector.tensor_copy, grouped, raws[c, a], 0, split)
+            interleave(nc.scalar.copy, grouped, raws[c, a], split, width)
+            for c0, piece in powers_of_two(width):
+                cols = slice(first + c0, first + c0 + piece)
+                nc.vector.quantize_mx(
+                    out=x_codes[a][:, cols].bitcast(FP8X4),
+                    scales=x_scales[a][:, cols],
+                    in_=grouped[:, c0 : c0 + piece, :].rearrange("p c i -> p (c i)"),
                 )
-            nc.scalar.activation(out=results[:, c0 : c0 + width], in_=sums, func=GELU, bias=bias[:, m : m + 1])
 
-        def place(m, results, h):
+        def place(m, first, width, tag):
+            results = keep.tile([P, width], F32, name=f"results_{m}_{first}", tag=tag)
+            for b0 in range(0, width, BANK):
+                run = min(BANK, width - b0)
+                sums = psum.tile([P, BANK], F32, name=f"sums_{m}_{first + b0}", tag=f"sums_{m}")
+                for c0, piece in powers_of_two(run):
+                    x_cols = slice(first + b0 + c0, first + b0 + c0 + piece)
+                    for a in range(PASSES):
+                        w_cols = slice(a * M + m * P, a * M + (m + 1) * P)
+                        nc.tensor.matmul_mx(
+                            out=sums[:, c0 : c0 + piece],
+                            lhsT=w_codes[:, w_cols].bitcast(FP8X4),
+                            lhsT_scale=w_scales[:, w_cols],
+                            rhs=x_codes[a][:, x_cols].bitcast(FP8X4),
+                            rhs_scale=x_scales[a][:, x_cols],
+                            start=(a == 0),
+                            stop=(a == PASSES - 1),
+                        )
+                row_bias = first_bias[:] if (m, first) == (0, 0) else bias[:, m : m + 1]
+                nc.scalar.activation(out=results[:, b0 : b0 + run], in_=sums[:, 0:run], func=GELU, bias=row_bias)
             nc.vector.tensor_tensor(
-                placed[m][:].indirect(offsets[:, h * LIST_COLUMNS : (h + 1) * LIST_COLUMNS]),
+                placed[m][:].indirect(offsets[:, first // LIST_ROWS : (first + width) // LIST_ROWS]),
                 results[:],
-                factors[h][:],
+                factor[:, first : first + width],
                 MULT,
             )
 
-        def first_row_tile(h):
-            results = keep.tile([P, HALF], F32, name=f"results_0_{h}", tag=f"last_{h}")
-            for block in BLOCKS[h]:
-                c0, width = block
-                if block == BLOCKS[h][-1]:
-                    sums = psum.tile([P, HALF], F32, name=f"sums_0_{h}_last", tag="late")
-                else:
-                    sums = psum.tile([P, BANK], F32, name=f"sums_0_{h}_{c0}", tag=f"sums_{c0}")
-                multiply(0, sums[:, 0:width], results, h, c0, width)
-            return results
-
-        def second_row_tile(h):
-            results = keep.tile([P, HALF], F32, name=f"results_1_{h}")
-            sums = psum.tile([P, HALF], F32, name=f"sums_1_{h}", tag="late")
-            for c0 in range(0, HALF, BANK):
-                multiply(1, sums[:, c0 : c0 + BANK], results, h, c0, BANK)
-            return results
-
-        whole, wide, narrow, last = LOADS[0]
-        copy_in(whole, 0, 512, 320)
-        quantize(whole, 0, 512)
-        copy_in(whole, 512, 1024, 320)
-        quantize(whole, 512, 1024)
-        copy_in(wide, 0, 512, 320)
-        quantize(wide, 0, 512)
-        copy_in(narrow, 0, 384, 224)
-        quantize(narrow, 0, 256)
-        quantize(narrow, 256, 384)
-        nc.scalar.copy(out=bias[:], in_=b_turned[:, 0:ROW_TILES])
-        copy_in(last, 0, 128, 64)
-        quantize(last, 0, 128)
-        place(0, first_row_tile(0), 0)
-        results = second_row_tile(0)
-
-        for load in LOADS[1]:
-            copy_in(load, 0, 512, 0)
-        quantize(LOADS[1][0], 0, 512)
-        place(1, results, 0)
-        quantize(LOADS[1][1], 0, 512)
-        quantize(LOADS[1][2], 0, 512)
-        quantize(LOADS[1][3], 0, 256)
-        quantize(LOADS[1][3], 256, 384)
-        quantize(LOADS[1][3], 384, 512)
-        place(0, first_row_tile(1), 1)
+        woven = len(LAGGING) - 1
+        last = len(CHUNKS) - 1
+        for c in range(len(CHUNKS)):
+            for a in range(PASSES):
+                prepare(c, a)
+            if 0 < c <= woven:
+                place(1, starts(LAGGING)[c - 1], LAGGING[c - 1], f"raw_{c}_{PASSES - 1}")
+            if c > woven:
+                place(0, starts(CHUNKS)[c - 1], CHUNKS[c - 1], f"raw_{c}_{PASSES - 1}")
+            if c < woven or c == last:
+                place(0, starts(CHUNKS)[c], CHUNKS[c], f"results_0_{c}")
         nc.sync.dma_start(out=out[0:P, :], in_=placed[0][:])
-        place(1, second_row_tile(1), 1)
+        place(1, starts(LAGGING)[woven], LAGGING[woven], "results_1_last")
         nc.sync.dma_start(out=out[P:M, :], in_=placed[1][:])

@@ -22,24 +22,16 @@ ROW_TILES = M // P
 BANK = 512
 LIST_ROWS = 16
 
-CHUNKS = [256] * 8
-FACTOR_LOADS = {0: 256, 1: 256, 2: 512, 4: 1024}
+CHUNK = 256
+CHUNKS = [CHUNK] * 8
+FACTOR_LOADS = {(1, 0): (0, 256), (1, 1): (256, 512), (2, 1): (512, 1024), (4, 1): (1024, 2048)}
 LAGGING = [256, 256, 256, 256, 256, 768]
-FIRST_VECTOR_COLUMNS = [128, 160]
+VECTOR_COLUMNS = {(0, 0): 128, (0, 1): 160, (1, 0): 256}
+AHEAD_FROM = 3
 
 
 def starts(widths):
     return [sum(widths[:i]) for i in range(len(widths))]
-
-
-def powers_of_two(width):
-    pieces = []
-    c0 = 0
-    for piece in (512, 256, 128):
-        while width - c0 >= piece:
-            pieces.append((c0, piece))
-            c0 += piece
-    return pieces
 
 
 def interleave(copy, grouped, raw, c0, c1):
@@ -66,9 +58,6 @@ def tile_list_hscat_gelu_kernel(tc, x, w, b, wgo, offs, out):
         table_loaded = keep.tile([P, 1], F32, name="table_loaded")
         nc.scalar.activation(out=table_loaded[:], in_=zero[:], func=GELU)
 
-        first_bias = keep.tile([P, 1], F32, name="first_bias", tag="grouped_1_0", align_bytes=64)
-        nc.scalar.copy(out=first_bias[:], in_=bias[:, 0:1])
-
         w_raw = []
         raws = {}
         factor = keep.tile([P, S], F32, name="factor")
@@ -88,12 +77,11 @@ def tile_list_hscat_gelu_kernel(tc, x, w, b, wgo, offs, out):
                     in_=x[a * K_PASS : (a + 1) * K_PASS, c0 : c0 + width].rearrange("(p i) c -> p i c", i=PACK),
                 )
                 raws[c, a] = raw
-            if c == 0:
-                nc.sync.dma_start(out=offsets[:], in_=offs)
-            if c in FACTOR_LOADS:
-                f0 = sum(run for chunk, run in FACTOR_LOADS.items() if chunk < c)
-                f1 = f0 + FACTOR_LOADS[c]
-                nc.sync.dma_start(out=factor[:, f0:f1], in_=wgo[:, f0:f1])
+                if (c, a) == (1, 0):
+                    nc.sync.dma_start(out=offsets[:], in_=offs)
+                if (c, a) in FACTOR_LOADS:
+                    f0, f1 = FACTOR_LOADS[c, a]
+                    nc.sync.dma_start(out=factor[:, f0:f1], in_=wgo[:, f0:f1])
 
         placed = [keep.tile([P, T], F32, name=f"placed_{m}") for m in range(ROW_TILES)]
         nc.vector.memset(placed[0][:, 0 : T // 2 - 1], 0.0)
@@ -111,44 +99,52 @@ def tile_list_hscat_gelu_kernel(tc, x, w, b, wgo, offs, out):
                 in_=w_grouped[:].rearrange("p n i -> p (n i)"),
             )
 
-        x_codes = [keep.tile([P, S], U32, name=f"x_codes_{a}", align_bytes=64) for a in range(PASSES)]
-        x_scales = [keep.tile([P, S], U8, name=f"x_scales_{a}", align_bytes=64) for a in range(PASSES)]
+        x_codes = [keep.tile([P, PASSES * CHUNK], U32, name=f"x_codes_{c}", align_bytes=64) for c in range(len(CHUNKS))]
+        x_scales = [keep.tile([P, PASSES * CHUNK], U8, name=f"x_scales_{c}", align_bytes=64) for c in range(len(CHUNKS))]
 
-        def prepare(c, a):
-            first, width = starts(CHUNKS)[c], CHUNKS[c]
-            grouped = keep.tile([P, width, PACK], BF16, name=f"grouped_{c}_{a}", tag=f"grouped_{c}_{a}", align_bytes=64)
-            split = FIRST_VECTOR_COLUMNS[a] if c == 0 else 0
-            if split > 0:
-                interleave(nc.vector.tensor_copy, grouped, raws[c, a], 0, split)
-            interleave(nc.scalar.copy, grouped, raws[c, a], split, width)
-            for c0, piece in powers_of_two(width):
-                cols = slice(first + c0, first + c0 + piece)
-                nc.vector.quantize_mx(
-                    out=x_codes[a][:, cols].bitcast(FP8X4),
-                    scales=x_scales[a][:, cols],
-                    in_=grouped[:, c0 : c0 + piece, :].rearrange("p c i -> p (c i)"),
-                )
+        def prepare(c):
+            grouped = keep.tile([P, PASSES * CHUNK, PACK], BF16, name=f"grouped_{c}", tag=f"grouped_{c}", align_bytes=64)
+            for a in range(PASSES):
+                cols = slice(a * CHUNK, (a + 1) * CHUNK)
+                split = VECTOR_COLUMNS.get((c, a), 0)
+                if split > 0:
+                    interleave(nc.vector.tensor_copy, grouped[:, cols, :], raws[c, a], 0, split)
+                if split < CHUNK:
+                    interleave(nc.scalar.copy, grouped[:, cols, :], raws[c, a], split, CHUNK)
+                if c == 0:
+                    quantize(c, grouped, cols)
+            if c > 0:
+                quantize(c, grouped, slice(0, PASSES * CHUNK))
+
+        def quantize(c, grouped, cols):
+            nc.vector.quantize_mx(
+                out=x_codes[c][:, cols].bitcast(FP8X4),
+                scales=x_scales[c][:, cols],
+                in_=grouped[:, cols, :].rearrange("p c i -> p (c i)"),
+            )
 
         def place(m, first, width, tag):
             results = keep.tile([P, width], F32, name=f"results_{m}_{first}", tag=tag)
             for b0 in range(0, width, BANK):
                 run = min(BANK, width - b0)
                 sums = psum.tile([P, BANK], F32, name=f"sums_{m}_{first + b0}", tag=f"sums_{m}")
-                for c0, piece in powers_of_two(run):
-                    x_cols = slice(first + b0 + c0, first + b0 + c0 + piece)
+                for c0 in range(0, run, CHUNK):
+                    c = (first + b0 + c0) // CHUNK
                     for a in range(PASSES):
+                        x_cols = slice(a * CHUNK, (a + 1) * CHUNK)
                         w_cols = slice(a * M + m * P, a * M + (m + 1) * P)
                         nc.tensor.matmul_mx(
-                            out=sums[:, c0 : c0 + piece],
+                            out=sums[:, c0 : c0 + CHUNK],
                             lhsT=w_codes[:, w_cols].bitcast(FP8X4),
                             lhsT_scale=w_scales[:, w_cols],
-                            rhs=x_codes[a][:, x_cols].bitcast(FP8X4),
-                            rhs_scale=x_scales[a][:, x_cols],
+                            rhs=x_codes[c][:, x_cols].bitcast(FP8X4),
+                            rhs_scale=x_scales[c][:, x_cols],
                             start=(a == 0),
                             stop=(a == PASSES - 1),
                         )
-                row_bias = first_bias[:] if (m, first) == (0, 0) else bias[:, m : m + 1]
-                nc.scalar.activation(out=results[:, b0 : b0 + run], in_=sums[:, 0:run], func=GELU, bias=row_bias)
+                nc.scalar.activation(
+                    out=results[:, b0 : b0 + run], in_=sums[:, 0:run], func=GELU, bias=bias[:, m : m + 1]
+                )
             nc.vector.tensor_tensor(
                 placed[m][:].indirect(offsets[:, first // LIST_ROWS : (first + width) // LIST_ROWS]),
                 results[:],
@@ -159,14 +155,18 @@ def tile_list_hscat_gelu_kernel(tc, x, w, b, wgo, offs, out):
         woven = len(LAGGING) - 1
         last = len(CHUNKS) - 1
         for c in range(len(CHUNKS)):
-            for a in range(PASSES):
-                prepare(c, a)
-            if 0 < c <= woven:
-                place(1, starts(LAGGING)[c - 1], LAGGING[c - 1], f"raw_{c}_{PASSES - 1}")
-            if c > woven:
-                place(0, starts(CHUNKS)[c - 1], CHUNKS[c - 1], f"raw_{c}_{PASSES - 1}")
-            if c < woven or c == last:
-                place(0, starts(CHUNKS)[c], CHUNKS[c], f"results_0_{c}")
+            prepare(c)
+            behind_copies = f"raw_{c}_{PASSES - 1}"
+            if 0 < c <= AHEAD_FROM:
+                place(1, (c - 1) * CHUNK, CHUNK, behind_copies)
+            if AHEAD_FROM < c < last:
+                place(0, (c - 1) * CHUNK, CHUNK, behind_copies)
+                if c < woven:
+                    place(1, (c - 1) * CHUNK, CHUNK, f"results_1_{c}")
+            if c < AHEAD_FROM:
+                place(0, c * CHUNK, CHUNK, f"results_0_{c}")
+        place(1, (woven - 1) * CHUNK, CHUNK, f"raw_{last}_{PASSES - 1}")
+        place(0, (last - 1) * CHUNK, 2 * CHUNK, "results_0_last")
         nc.sync.dma_start(out=out[0:P, :], in_=placed[0][:])
         place(1, starts(LAGGING)[woven], LAGGING[woven], "results_1_last")
         nc.sync.dma_start(out=out[P:M, :], in_=placed[1][:])

@@ -24,10 +24,11 @@ LIST_ROWS = 16
 
 CHUNK = 256
 CHUNKS = [CHUNK] * 8
-FACTOR_LOADS = {(1, 0): (0, 256), (1, 1): (256, 512), (2, 1): (512, 1024), (4, 1): (1024, 2048)}
+FACTOR_LOADS = {(1, 0): (0, 256), (1, 1): (256, 768), (3, 1): (768, 1536), (7, 1): (1536, 2048)}
 LAGGING = [256, 256, 256, 256, 256, 768]
 VECTOR_COLUMNS = {(0, 0): 128, (0, 1): 160, (1, 0): 256}
 AHEAD_FROM = 3
+PAIRED = ()
 
 
 def starts(widths):
@@ -71,12 +72,20 @@ def tile_list_hscat_gelu_kernel(tc, x, w, b, wgo, offs, out):
                     )
                     w_raw.append(rows)
             for a in range(PASSES):
-                raw = keep.tile([P, PACK, width], F32, name=f"raw_{c}_{a}", tag=f"raw_{c}_{a}")
+                if (c, a) in raws:
+                    continue
+                chunks = 2 if a == 0 and c in PAIRED else 1
+                raw = keep.tile(
+                    [P, PACK, chunks * width], F32, name=f"raw_{c}_{a}", tag=f"raw_{c}_{a}", align_bytes=64
+                )
                 nc.sync.dma_start(
                     out=raw[:],
-                    in_=x[a * K_PASS : (a + 1) * K_PASS, c0 : c0 + width].rearrange("(p i) c -> p i c", i=PACK),
+                    in_=x[a * K_PASS : (a + 1) * K_PASS, c0 : c0 + chunks * width].rearrange(
+                        "(p i) c -> p i c", i=PACK
+                    ),
                 )
-                raws[c, a] = raw
+                for later in range(chunks):
+                    raws[c + later, a] = raw[:, :, later * width : (later + 1) * width]
                 if (c, a) == (1, 0):
                     nc.sync.dma_start(out=offsets[:], in_=offs)
                 if (c, a) in FACTOR_LOADS:
@@ -102,29 +111,41 @@ def tile_list_hscat_gelu_kernel(tc, x, w, b, wgo, offs, out):
         x_codes = [keep.tile([P, PASSES * CHUNK], U32, name=f"x_codes_{c}", align_bytes=64) for c in range(len(CHUNKS))]
         x_scales = [keep.tile([P, PASSES * CHUNK], U8, name=f"x_scales_{c}", align_bytes=64) for c in range(len(CHUNKS))]
 
-        def prepare(c):
-            grouped = keep.tile([P, PASSES * CHUNK, PACK], BF16, name=f"grouped_{c}", tag=f"grouped_{c}", align_bytes=64)
-            for a in range(PASSES):
-                cols = slice(a * CHUNK, (a + 1) * CHUNK)
-                split = VECTOR_COLUMNS.get((c, a), 0)
-                if split > 0:
-                    interleave(nc.vector.tensor_copy, grouped[:, cols, :], raws[c, a], 0, split)
-                if split < CHUNK:
-                    interleave(nc.scalar.copy, grouped[:, cols, :], raws[c, a], split, CHUNK)
-                if c == 0:
-                    quantize(c, grouped, cols)
-            if c > 0:
-                quantize(c, grouped, slice(0, PASSES * CHUNK))
+        early_bias = {}
+        for c in range(AHEAD_FROM):
+            held = keep.tile([P, 1], F32, name=f"early_bias_{c}", tag=f"grouped_{c + 1}_1", align_bytes=64)
+            nc.scalar.copy(out=held[:], in_=bias[:, 0:1])
+            early_bias[0, c * CHUNK] = held[:]
 
-        def quantize(c, grouped, cols):
+        def runs_of(c):
+            return [[a] for a in range(PASSES)] if c <= AHEAD_FROM else [list(range(PASSES))]
+
+        grouped = {}
+
+        def copy_in(c, a):
+            run = [run for run in runs_of(c) if a in run][0]
+            tag = f"grouped_{c}_{run[-1]}"
+            if tag not in grouped:
+                grouped[tag] = keep.tile([P, len(run) * CHUNK, PACK], BF16, name=tag, tag=tag, align_bytes=64)
+            i = run.index(a)
+            part = grouped[tag][:, i * CHUNK : (i + 1) * CHUNK, :]
+            split = VECTOR_COLUMNS.get((c, a), 0)
+            if split > 0:
+                interleave(nc.vector.tensor_copy, part, raws[c, a], 0, split)
+            if split < CHUNK:
+                interleave(nc.scalar.copy, part, raws[c, a], split, CHUNK)
+
+        def quantize(c, run):
+            cols = slice(run[0] * CHUNK, (run[-1] + 1) * CHUNK)
             nc.vector.quantize_mx(
                 out=x_codes[c][:, cols].bitcast(FP8X4),
                 scales=x_scales[c][:, cols],
-                in_=grouped[:, cols, :].rearrange("p c i -> p (c i)"),
+                in_=grouped[f"grouped_{c}_{run[-1]}"][:].rearrange("p c i -> p (c i)"),
             )
 
         def place(m, first, width, tag):
-            results = keep.tile([P, width], F32, name=f"results_{m}_{first}", tag=tag)
+            results = keep.tile([P, width], F32, name=f"results_{m}_{first}", tag=tag, align_bytes=64)
+            row_bias = early_bias.get((m, first), bias[:, m : m + 1])
             for b0 in range(0, width, BANK):
                 run = min(BANK, width - b0)
                 sums = psum.tile([P, BANK], F32, name=f"sums_{m}_{first + b0}", tag=f"sums_{m}")
@@ -143,7 +164,7 @@ def tile_list_hscat_gelu_kernel(tc, x, w, b, wgo, offs, out):
                             stop=(a == PASSES - 1),
                         )
                 nc.scalar.activation(
-                    out=results[:, b0 : b0 + run], in_=sums[:, 0:run], func=GELU, bias=bias[:, m : m + 1]
+                    out=results[:, b0 : b0 + run], in_=sums[:, 0:run], func=GELU, bias=row_bias
                 )
             nc.vector.tensor_tensor(
                 placed[m][:].indirect(offsets[:, first // LIST_ROWS : (first + width) // LIST_ROWS]),
@@ -155,18 +176,21 @@ def tile_list_hscat_gelu_kernel(tc, x, w, b, wgo, offs, out):
         woven = len(LAGGING) - 1
         last = len(CHUNKS) - 1
         for c in range(len(CHUNKS)):
-            prepare(c)
+            for run in runs_of(c):
+                for a in run:
+                    copy_in(c, a)
+                    if a == 0 and AHEAD_FROM + 1 < c <= woven:
+                        place(1, (c - 2) * CHUNK, CHUNK, f"raw_{c}_0")
+                quantize(c, run)
             behind_copies = f"raw_{c}_{PASSES - 1}"
             if 0 < c <= AHEAD_FROM:
                 place(1, (c - 1) * CHUNK, CHUNK, behind_copies)
             if AHEAD_FROM < c < last:
                 place(0, (c - 1) * CHUNK, CHUNK, behind_copies)
-                if c < woven:
-                    place(1, (c - 1) * CHUNK, CHUNK, f"results_1_{c}")
             if c < AHEAD_FROM:
                 place(0, c * CHUNK, CHUNK, f"results_0_{c}")
         place(1, (woven - 1) * CHUNK, CHUNK, f"raw_{last}_{PASSES - 1}")
         place(0, (last - 1) * CHUNK, 2 * CHUNK, "results_0_last")
         nc.sync.dma_start(out=out[0:P, :], in_=placed[0][:])
-        place(1, starts(LAGGING)[woven], LAGGING[woven], "results_1_last")
+        place(1, starts(LAGGING)[woven], LAGGING[woven], f"grouped_{last}_1")
         nc.sync.dma_start(out=out[P:M, :], in_=placed[1][:])

@@ -20,33 +20,37 @@ K_PASS = P * PACK
 PASSES = K // K_PASS
 ROW_TILES = M // P
 BANK = 512
+PSUM_TURNS = 3
 LIST_ROWS = 16
 
 CHUNK = 256
-CHUNKS = [CHUNK] * 8
-FACTOR_LOADS = {(1, 0): (0, 256), (1, 1): (256, 768), (3, 1): (768, 1536), (7, 1): (1536, 2048)}
-LAGGING = [256, 256, 256, 256, 256, 768]
-VECTOR_COLUMNS = {(0, 0): 128, (0, 1): 160, (1, 0): 256}
+CHUNKS = S // CHUNK
+KEPT_BACK = 3
 AHEAD_FROM = 3
-PAIRED = ()
 
-
-def starts(widths):
-    return [sum(widths[:i]) for i in range(len(widths))]
+VECTOR_COLUMNS = {(0, 0): 128, (0, 1): 160, (1, 0): 256}
+PASS_BY_PASS = (0, 1)
+FACTOR_LOADS = {(1, 0): (0, 256), (1, 1): (256, 512), (2, 1): (512, 1024), (4, 1): (1024, 1536), (7, 1): (1536, 2048)}
 
 
 def interleave(copy, grouped, raw, c0, c1):
     copy(
-        out=grouped[:, c0:c1, :].rearrange("p (c i) j -> p c j i", i=4),
-        in_=raw[:, :, c0:c1].rearrange("p j (c i) -> p c j i", i=4),
+        out=grouped[:, c0:c1, :].rearrange("p (c i) j -> p c j i", i=2),
+        in_=raw[:, :, c0:c1].rearrange("p j (c i) -> p c j i", i=2),
     )
+
+
+def passes_together(c):
+    if c in PASS_BY_PASS:
+        return [[a] for a in range(PASSES)]
+    return [list(range(PASSES))]
 
 
 def tile_list_hscat_gelu_kernel(tc, x, w, b, wgo, offs, out):
     nc = tc.nc
     with ExitStack() as ctx:
         keep = ctx.enter_context(tc.tile_pool(name="keep", bufs=1))
-        psum = ctx.enter_context(tc.psum_pool(name="psum", bufs=3))
+        psum = ctx.enter_context(tc.psum_pool(name="psum", bufs=PSUM_TURNS))
 
         offsets = keep.tile([P, S // LIST_ROWS], U16, name="offsets")
 
@@ -60,42 +64,35 @@ def tile_list_hscat_gelu_kernel(tc, x, w, b, wgo, offs, out):
         nc.scalar.activation(out=table_loaded[:], in_=zero[:], func=GELU)
 
         w_raw = []
-        raws = {}
+        for a in range(PASSES):
+            rows = keep.tile([P, PACK, M], F32, name=f"w_raw_{a}")
+            nc.sync.dma_start(
+                out=rows[:].rearrange("p i n -> p (i n)"),
+                in_=w[a * K_PASS : (a + 1) * K_PASS, :].rearrange("(p i) n -> p (i n)", i=PACK),
+            )
+            w_raw.append(rows)
+        x_raw = {}
         factor = keep.tile([P, S], F32, name="factor")
-        for c, (c0, width) in enumerate(zip(starts(CHUNKS), CHUNKS)):
+        for c in range(CHUNKS):
             for a in range(PASSES):
-                if c == 0:
-                    rows = keep.tile([P, PACK, M], F32, name=f"w_raw_{a}")
-                    nc.sync.dma_start(
-                        out=rows[:].rearrange("p i n -> p (i n)"),
-                        in_=w[a * K_PASS : (a + 1) * K_PASS, :].rearrange("(p i) n -> p (i n)", i=PACK),
-                    )
-                    w_raw.append(rows)
-            for a in range(PASSES):
-                if (c, a) in raws:
-                    continue
-                chunks = 2 if a == 0 and c in PAIRED else 1
-                raw = keep.tile(
-                    [P, PACK, chunks * width], F32, name=f"raw_{c}_{a}", tag=f"raw_{c}_{a}", align_bytes=64
-                )
+                rows = keep.tile([P, PACK, CHUNK], F32, name=f"raw_{c}_{a}", tag=f"raw_{c}_{a}", align_bytes=64)
                 nc.sync.dma_start(
-                    out=raw[:],
-                    in_=x[a * K_PASS : (a + 1) * K_PASS, c0 : c0 + chunks * width].rearrange(
+                    out=rows[:],
+                    in_=x[a * K_PASS : (a + 1) * K_PASS, c * CHUNK : (c + 1) * CHUNK].rearrange(
                         "(p i) c -> p i c", i=PACK
                     ),
                 )
-                for later in range(chunks):
-                    raws[c + later, a] = raw[:, :, later * width : (later + 1) * width]
-                if (c, a) == (1, 0):
-                    nc.sync.dma_start(out=offsets[:], in_=offs)
+                x_raw[c, a] = rows
                 if (c, a) in FACTOR_LOADS:
                     f0, f1 = FACTOR_LOADS[c, a]
+                    if f0 == 0:
+                        nc.sync.dma_start(out=offsets[:], in_=offs)
                     nc.sync.dma_start(out=factor[:, f0:f1], in_=wgo[:, f0:f1])
 
-        placed = [keep.tile([P, T], F32, name=f"placed_{m}") for m in range(ROW_TILES)]
-        nc.vector.memset(placed[0][:, 0 : T // 2 - 1], 0.0)
-        nc.vector.memset(placed[0][:, T // 2 - 1 : T], 0.0)
-        nc.gpsimd.memset(placed[1][:], 0.0)
+        windows = [keep.tile([P, T], F32, name=f"window_{m}") for m in range(ROW_TILES)]
+        nc.vector.memset(windows[0][:], 0.0)
+        nc.gpsimd.memset(windows[1][:, 0 : T // 2], 0.0)
+        nc.vector.memset(windows[1][:, T // 2 : T], 0.0)
 
         w_codes = keep.tile([P, PASSES * M], U32, name="w_codes", align_bytes=64)
         w_scales = keep.tile([P, PASSES * M], U8, name="w_scales", align_bytes=64)
@@ -108,49 +105,28 @@ def tile_list_hscat_gelu_kernel(tc, x, w, b, wgo, offs, out):
                 in_=w_grouped[:].rearrange("p n i -> p (n i)"),
             )
 
-        x_codes = [keep.tile([P, PASSES * CHUNK], U32, name=f"x_codes_{c}", align_bytes=64) for c in range(len(CHUNKS))]
-        x_scales = [keep.tile([P, PASSES * CHUNK], U8, name=f"x_scales_{c}", align_bytes=64) for c in range(len(CHUNKS))]
+        x_codes = [keep.tile([P, PASSES * CHUNK], U32, name=f"x_codes_{c}", align_bytes=64) for c in range(CHUNKS)]
+        x_scales = [keep.tile([P, PASSES * CHUNK], U8, name=f"x_scales_{c}", align_bytes=64) for c in range(CHUNKS)]
 
-        early_bias = {}
-        for c in range(AHEAD_FROM):
-            held = keep.tile([P, 1], F32, name=f"early_bias_{c}", tag=f"grouped_{c + 1}_1", align_bytes=64)
-            nc.scalar.copy(out=held[:], in_=bias[:, 0:1])
-            early_bias[0, c * CHUNK] = held[:]
+        first_bias = keep.tile([P, 1], F32, name="first_bias", tag="first_bias", align_bytes=64)
+        nc.scalar.copy(out=first_bias[:], in_=bias[:, 0:1])
 
-        def runs_of(c):
-            return [[a] for a in range(PASSES)] if c <= AHEAD_FROM else [list(range(PASSES))]
-
-        grouped = {}
-
-        def copy_in(c, a):
-            run = [run for run in runs_of(c) if a in run][0]
-            tag = f"grouped_{c}_{run[-1]}"
-            if tag not in grouped:
-                grouped[tag] = keep.tile([P, len(run) * CHUNK, PACK], BF16, name=tag, tag=tag, align_bytes=64)
-            i = run.index(a)
-            part = grouped[tag][:, i * CHUNK : (i + 1) * CHUNK, :]
+        def copy_in(grouped, c, a):
             split = VECTOR_COLUMNS.get((c, a), 0)
             if split > 0:
-                interleave(nc.vector.tensor_copy, part, raws[c, a], 0, split)
+                interleave(nc.vector.tensor_copy, grouped, x_raw[c, a], 0, split)
             if split < CHUNK:
-                interleave(nc.scalar.copy, part, raws[c, a], split, CHUNK)
+                interleave(nc.scalar.copy, grouped, x_raw[c, a], split, CHUNK)
 
-        def quantize(c, run):
-            cols = slice(run[0] * CHUNK, (run[-1] + 1) * CHUNK)
-            nc.vector.quantize_mx(
-                out=x_codes[c][:, cols].bitcast(FP8X4),
-                scales=x_scales[c][:, cols],
-                in_=grouped[f"grouped_{c}_{run[-1]}"][:].rearrange("p c i -> p (c i)"),
-            )
-
-        def place(m, first, width, tag):
-            results = keep.tile([P, width], F32, name=f"results_{m}_{first}", tag=tag, align_bytes=64)
-            row_bias = early_bias.get((m, first), bias[:, m : m + 1])
+        def place(m, first, count, slot):
+            width = count * CHUNK
+            results = keep.tile([P, width], F32, name=f"results_{m}_{first}", tag=slot, align_bytes=64)
+            row_bias = first_bias[:] if (m, first) == (0, 0) else bias[:, m : m + 1]
             for b0 in range(0, width, BANK):
                 run = min(BANK, width - b0)
-                sums = psum.tile([P, BANK], F32, name=f"sums_{m}_{first + b0}", tag=f"sums_{m}")
+                sums = psum.tile([P, BANK], F32, name=f"sums_{m}_{first}_{b0}", tag=f"sums_{m}")
                 for c0 in range(0, run, CHUNK):
-                    c = (first + b0 + c0) // CHUNK
+                    c = first + (b0 + c0) // CHUNK
                     for a in range(PASSES):
                         x_cols = slice(a * CHUNK, (a + 1) * CHUNK)
                         w_cols = slice(a * M + m * P, a * M + (m + 1) * P)
@@ -163,34 +139,39 @@ def tile_list_hscat_gelu_kernel(tc, x, w, b, wgo, offs, out):
                             start=(a == 0),
                             stop=(a == PASSES - 1),
                         )
-                nc.scalar.activation(
-                    out=results[:, b0 : b0 + run], in_=sums[:, 0:run], func=GELU, bias=row_bias
-                )
+                nc.scalar.activation(out=results[:, b0 : b0 + run], in_=sums[:, 0:run], func=GELU, bias=row_bias)
+            j0 = first * CHUNK
             nc.vector.tensor_tensor(
-                placed[m][:].indirect(offsets[:, first // LIST_ROWS : (first + width) // LIST_ROWS]),
+                windows[m][:].indirect(offsets[:, j0 // LIST_ROWS : (j0 + width) // LIST_ROWS]),
                 results[:],
-                factor[:, first : first + width],
+                factor[:, j0 : j0 + width],
                 MULT,
             )
 
-        woven = len(LAGGING) - 1
-        last = len(CHUNKS) - 1
-        for c in range(len(CHUNKS)):
-            for run in runs_of(c):
-                for a in run:
-                    copy_in(c, a)
-                    if a == 0 and AHEAD_FROM + 1 < c <= woven:
-                        place(1, (c - 2) * CHUNK, CHUNK, f"raw_{c}_0")
-                quantize(c, run)
-            behind_copies = f"raw_{c}_{PASSES - 1}"
-            if 0 < c <= AHEAD_FROM:
-                place(1, (c - 1) * CHUNK, CHUNK, behind_copies)
-            if AHEAD_FROM < c < last:
-                place(0, (c - 1) * CHUNK, CHUNK, behind_copies)
+        woven = CHUNKS - KEPT_BACK
+        last = CHUNKS - 1
+        for c in range(CHUNKS):
+            for group in passes_together(c):
+                name = f"grouped_{c}_{group[-1]}"
+                slot = "first_bias" if (c, group[0]) == (1, 1) else name
+                grouped = keep.tile([P, len(group) * CHUNK, PACK], BF16, name=name, tag=slot, align_bytes=64)
+                for i, a in enumerate(group):
+                    copy_in(grouped[:, i * CHUNK : (i + 1) * CHUNK, :], c, a)
+                    if a == 0 and AHEAD_FROM <= c - 2 < woven:
+                        place(1, c - 2, 1, f"raw_{c}_0")
+                cols = slice(group[0] * CHUNK, (group[-1] + 1) * CHUNK)
+                nc.vector.quantize_mx(
+                    out=x_codes[c][:, cols].bitcast(FP8X4),
+                    scales=x_scales[c][:, cols],
+                    in_=grouped[:].rearrange("p c i -> p (c i)"),
+                )
+            if 0 <= c - 1 < AHEAD_FROM:
+                place(1, c - 1, 1, f"raw_{c}_1")
             if c < AHEAD_FROM:
-                place(0, c * CHUNK, CHUNK, f"results_0_{c}")
-        place(1, (woven - 1) * CHUNK, CHUNK, f"raw_{last}_{PASSES - 1}")
-        place(0, (last - 1) * CHUNK, 2 * CHUNK, "results_0_last")
-        nc.sync.dma_start(out=out[0:P, :], in_=placed[0][:])
-        place(1, starts(LAGGING)[woven], LAGGING[woven], f"grouped_{last}_1")
-        nc.sync.dma_start(out=out[P:M, :], in_=placed[1][:])
+                place(0, c, 1, f"results_0_{c}")
+            if c - 1 >= AHEAD_FROM:
+                place(0, c - 1, 1, f"raw_{c}_1")
+        place(0, last, 1, "results_0_last")
+        nc.sync.dma_start(out=out[0:P, :], in_=windows[0][:])
+        place(1, woven, KEPT_BACK, f"grouped_{last}_1")
+        nc.sync.dma_start(out=out[P:M, :], in_=windows[1][:])

@@ -30,7 +30,16 @@ AHEAD_FROM = 3
 
 VECTOR_COLUMNS = {(0, 0): 128, (0, 1): 160, (1, 0): 256}
 PASS_BY_PASS = (0, 1)
-FACTOR_LOADS = {(1, 0): (0, 256), (1, 1): (256, 512), (2, 1): (512, 1024), (4, 1): (1024, 1536), (7, 1): (1536, 2048)}
+FACTOR_LOADS = {
+    (1, 0): (0, 256),
+    (2, 0): (256, 512),
+    (3, 1): (512, 768),
+    (4, 1): (768, 1024),
+    (5, 1): (1024, 1536),
+    (7, 1): (1536, 2048),
+}
+LOADED_IN_HALVES = ((1, 1),)
+COPIED_IN_HALVES = ((2, 0), (3, 0))
 
 
 def interleave(copy, grouped, raw, c0, c1):
@@ -75,14 +84,17 @@ def tile_list_hscat_gelu_kernel(tc, x, w, b, wgo, offs, out):
         factor = keep.tile([P, S], F32, name="factor")
         for c in range(CHUNKS):
             for a in range(PASSES):
-                rows = keep.tile([P, PACK, CHUNK], F32, name=f"raw_{c}_{a}", tag=f"raw_{c}_{a}", align_bytes=64)
-                nc.sync.dma_start(
-                    out=rows[:],
-                    in_=x[a * K_PASS : (a + 1) * K_PASS, c * CHUNK : (c + 1) * CHUNK].rearrange(
-                        "(p i) c -> p i c", i=PACK
-                    ),
-                )
-                x_raw[c, a] = rows
+                width = CHUNK // 2 if (c, a) in LOADED_IN_HALVES else CHUNK
+                x_raw[c, a] = []
+                for c0 in range(0, CHUNK, width):
+                    name = f"raw_{c}_{a}" if c0 == 0 else f"raw_{c}_{a}_second"
+                    rows = keep.tile([P, PACK, width], F32, name=name, tag=name, align_bytes=64)
+                    j0 = c * CHUNK + c0
+                    nc.sync.dma_start(
+                        out=rows[:],
+                        in_=x[a * K_PASS : (a + 1) * K_PASS, j0 : j0 + width].rearrange("(p i) c -> p i c", i=PACK),
+                    )
+                    x_raw[c, a].append(rows)
                 if (c, a) in FACTOR_LOADS:
                     f0, f1 = FACTOR_LOADS[c, a]
                     if f0 == 0:
@@ -112,11 +124,21 @@ def tile_list_hscat_gelu_kernel(tc, x, w, b, wgo, offs, out):
         nc.scalar.copy(out=first_bias[:], in_=bias[:, 0:1])
 
         def copy_in(grouped, c, a):
+            half = CHUNK // 2
+            if (c, a) in LOADED_IN_HALVES:
+                for h in range(2):
+                    interleave(nc.scalar.copy, grouped[:, h * half : (h + 1) * half, :], x_raw[c, a][h], 0, half)
+                return
+            raw = x_raw[c, a][0]
+            if (c, a) in COPIED_IN_HALVES:
+                interleave(nc.scalar.copy, grouped, raw, 0, half)
+                interleave(nc.scalar.copy, grouped, raw, half, CHUNK)
+                return
             split = VECTOR_COLUMNS.get((c, a), 0)
             if split > 0:
-                interleave(nc.vector.tensor_copy, grouped, x_raw[c, a], 0, split)
+                interleave(nc.vector.tensor_copy, grouped, raw, 0, split)
             if split < CHUNK:
-                interleave(nc.scalar.copy, grouped, x_raw[c, a], split, CHUNK)
+                interleave(nc.scalar.copy, grouped, raw, split, CHUNK)
 
         def place(m, first, count, slot):
             width = count * CHUNK
@@ -158,7 +180,7 @@ def tile_list_hscat_gelu_kernel(tc, x, w, b, wgo, offs, out):
                 for i, a in enumerate(group):
                     copy_in(grouped[:, i * CHUNK : (i + 1) * CHUNK, :], c, a)
                     if a == 0 and AHEAD_FROM <= c - 2 < woven:
-                        place(1, c - 2, 1, f"raw_{c}_0")
+                        place(1, c - 2, 1, f"raw_{c - 1}_1")
                 cols = slice(group[0] * CHUNK, (group[-1] + 1) * CHUNK)
                 nc.vector.quantize_mx(
                     out=x_codes[c][:, cols].bitcast(FP8X4),
@@ -166,11 +188,11 @@ def tile_list_hscat_gelu_kernel(tc, x, w, b, wgo, offs, out):
                     in_=grouped[:].rearrange("p c i -> p (c i)"),
                 )
             if 0 <= c - 1 < AHEAD_FROM:
-                place(1, c - 1, 1, f"raw_{c}_1")
+                place(1, c - 1, 1, {1: "raw_1_1_second", 2: "raw_2_1", 3: "raw_3_0"}[c])
             if c < AHEAD_FROM:
                 place(0, c, 1, f"results_0_{c}")
             if c - 1 >= AHEAD_FROM:
-                place(0, c - 1, 1, f"raw_{c}_1")
+                place(0, c - 1, 1, f"raw_{c}_0")
         place(0, last, 1, "results_0_last")
         nc.sync.dma_start(out=out[0:P, :], in_=windows[0][:])
         place(1, woven, KEPT_BACK, f"grouped_{last}_1")

@@ -24,22 +24,21 @@ PSUM_TURNS = 3
 LIST_ROWS = 16
 
 CHUNK = 256
+HALF = CHUNK // 2
 CHUNKS = S // CHUNK
+LAST = CHUNKS - 1
 KEPT_BACK = 3
 AHEAD_FROM = 3
 
-VECTOR_COLUMNS = {(0, 0): 128, (0, 1): 160, (1, 0): 256}
-PASS_BY_PASS = (0, 1)
+VECTOR_COLUMNS = (128, 160)
 FACTOR_LOADS = {
     (1, 0): (0, 256),
-    (2, 0): (256, 512),
+    (1, 1): (256, 512),
     (3, 1): (512, 768),
     (4, 1): (768, 1024),
     (5, 1): (1024, 1536),
     (7, 1): (1536, 2048),
 }
-LOADED_IN_HALVES = ((1, 1),)
-COPIED_IN_HALVES = ((2, 0), (3, 0))
 
 
 def interleave(copy, grouped, raw, c0, c1):
@@ -47,12 +46,6 @@ def interleave(copy, grouped, raw, c0, c1):
         out=grouped[:, c0:c1, :].rearrange("p (c i) j -> p c j i", i=2),
         in_=raw[:, :, c0:c1].rearrange("p j (c i) -> p c j i", i=2),
     )
-
-
-def passes_together(c):
-    if c in PASS_BY_PASS:
-        return [[a] for a in range(PASSES)]
-    return [list(range(PASSES))]
 
 
 def tile_list_hscat_gelu_kernel(tc, x, w, b, wgo, offs, out):
@@ -84,7 +77,7 @@ def tile_list_hscat_gelu_kernel(tc, x, w, b, wgo, offs, out):
         factor = keep.tile([P, S], F32, name="factor")
         for c in range(CHUNKS):
             for a in range(PASSES):
-                width = CHUNK // 2 if (c, a) in LOADED_IN_HALVES else CHUNK
+                width = HALF if (c, a) == (1, 1) else CHUNK
                 x_raw[c, a] = []
                 for c0 in range(0, CHUNK, width):
                     name = f"raw_{c}_{a}" if c0 == 0 else f"raw_{c}_{a}_second"
@@ -123,29 +116,26 @@ def tile_list_hscat_gelu_kernel(tc, x, w, b, wgo, offs, out):
         first_bias = keep.tile([P, 1], F32, name="first_bias", tag="first_bias", align_bytes=64)
         nc.scalar.copy(out=first_bias[:], in_=bias[:, 0:1])
 
-        def copy_in(grouped, c, a):
-            half = CHUNK // 2
-            if (c, a) in LOADED_IN_HALVES:
-                for h in range(2):
-                    interleave(nc.scalar.copy, grouped[:, h * half : (h + 1) * half, :], x_raw[c, a][h], 0, half)
-                return
-            raw = x_raw[c, a][0]
-            if (c, a) in COPIED_IN_HALVES:
-                interleave(nc.scalar.copy, grouped, raw, 0, half)
-                interleave(nc.scalar.copy, grouped, raw, half, CHUNK)
-                return
-            split = VECTOR_COLUMNS.get((c, a), 0)
-            if split > 0:
-                interleave(nc.vector.tensor_copy, grouped, raw, 0, split)
-            if split < CHUNK:
-                interleave(nc.scalar.copy, grouped, raw, split, CHUNK)
+        def interleaved(c, passes, slot):
+            return keep.tile([P, passes * CHUNK, PACK], BF16, name=f"grouped_{c}_{slot}", tag=slot, align_bytes=64)
 
-        def place(m, first, count, slot):
+        def copy_pass(copy, grouped, c, a, c0=0, c1=CHUNK):
+            interleave(copy, grouped[:, a * CHUNK : (a + 1) * CHUNK, :], x_raw[c, a][0], c0, c1)
+
+        def quantise(c, grouped, first_pass=0):
+            cols = slice(first_pass * CHUNK, first_pass * CHUNK + grouped.shape[1])
+            nc.vector.quantize_mx(
+                out=x_codes[c][:, cols].bitcast(FP8X4),
+                scales=x_scales[c][:, cols],
+                in_=grouped[:].rearrange("p c i -> p (c i)"),
+            )
+
+        def place(m, first, count, slot, step=BANK):
             width = count * CHUNK
             results = keep.tile([P, width], F32, name=f"results_{m}_{first}", tag=slot, align_bytes=64)
             row_bias = first_bias[:] if (m, first) == (0, 0) else bias[:, m : m + 1]
-            for b0 in range(0, width, BANK):
-                run = min(BANK, width - b0)
+            for b0 in range(0, width, step):
+                run = min(step, width - b0)
                 sums = psum.tile([P, BANK], F32, name=f"sums_{m}_{first}_{b0}", tag=f"sums_{m}")
                 for c0 in range(0, run, CHUNK):
                     c = first + (b0 + c0) // CHUNK
@@ -170,30 +160,55 @@ def tile_list_hscat_gelu_kernel(tc, x, w, b, wgo, offs, out):
                 MULT,
             )
 
-        woven = CHUNKS - KEPT_BACK
-        last = CHUNKS - 1
-        for c in range(CHUNKS):
-            for group in passes_together(c):
-                name = f"grouped_{c}_{group[-1]}"
-                slot = "first_bias" if (c, group[0]) == (1, 1) else name
-                grouped = keep.tile([P, len(group) * CHUNK, PACK], BF16, name=name, tag=slot, align_bytes=64)
-                for i, a in enumerate(group):
-                    copy_in(grouped[:, i * CHUNK : (i + 1) * CHUNK, :], c, a)
-                    if a == 0 and AHEAD_FROM <= c - 2 < woven:
-                        place(1, c - 2, 1, f"raw_{c - 1}_1")
-                cols = slice(group[0] * CHUNK, (group[-1] + 1) * CHUNK)
-                nc.vector.quantize_mx(
-                    out=x_codes[c][:, cols].bitcast(FP8X4),
-                    scales=x_scales[c][:, cols],
-                    in_=grouped[:].rearrange("p c i -> p (c i)"),
-                )
-            if 0 <= c - 1 < AHEAD_FROM:
-                place(1, c - 1, 1, {1: "raw_1_1_second", 2: "raw_2_1", 3: "raw_3_0"}[c])
-            if c < AHEAD_FROM:
-                place(0, c, 1, f"results_0_{c}")
-            if c - 1 >= AHEAD_FROM:
+
+        for a in range(PASSES):
+            grouped = interleaved(0, 1, f"grouped_0_{a}")
+            interleave(nc.vector.tensor_copy, grouped, x_raw[0, a][0], 0, VECTOR_COLUMNS[a])
+            interleave(nc.scalar.copy, grouped, x_raw[0, a][0], VECTOR_COLUMNS[a], CHUNK)
+            quantise(0, grouped, a)
+        place(0, 0, 1, "results_0_0")
+        grouped = interleaved(1, 1, "grouped_1_0")
+        interleave(nc.vector.tensor_copy, grouped, x_raw[1, 0][0], 0, CHUNK)
+        quantise(1, grouped, 0)
+        grouped = interleaved(1, 1, "first_bias")
+        for h in range(2):
+            interleave(nc.scalar.copy, grouped[:, h * HALF : (h + 1) * HALF, :], x_raw[1, 1][h], 0, HALF)
+        quantise(1, grouped, 1)
+        place(1, 0, 1, "raw_1_1")
+        place(0, 1, 1, "results_0_1")
+
+        grouped = interleaved(2, 1, "grouped_2_0")
+        interleave(nc.scalar.copy, grouped, x_raw[2, 0][0], 0, HALF)
+        interleave(nc.scalar.copy, grouped, x_raw[2, 0][0], HALF, CHUNK)
+        quantise(2, grouped, 0)
+        grouped = interleaved(2, 1, "grouped_2_1")
+        interleave(nc.scalar.copy, grouped, x_raw[2, 1][0], 0, CHUNK)
+        quantise(2, grouped, 1)
+        place(1, 1, 1, "raw_2_0")
+        place(0, 2, 1, "results_0_2")
+
+        for c in range(AHEAD_FROM, LAST):
+            grouped = interleaved(c, PASSES, f"grouped_{c}")
+            copy_pass(nc.scalar.copy, grouped, c, 0)
+            if c == AHEAD_FROM + 2:
+                place(1, AHEAD_FROM, 1, f"raw_{c - 1}_1")
+            copy_pass(nc.scalar.copy, grouped, c, 1)
+            quantise(c, grouped)
+            if c == AHEAD_FROM:
+                place(1, c - 1, 1, f"raw_{c}_0")
+            elif c < LAST - 1:
                 place(0, c - 1, 1, f"raw_{c}_0")
-        place(0, last, 1, "results_0_last")
+
+        grouped = interleaved(LAST, 1, "grouped_last_0")
+        interleave(nc.scalar.copy, grouped, x_raw[LAST, 0][0], 0, HALF)
+        place(0, LAST - 2, 1, f"raw_{LAST - 1}_1")
+        interleave(nc.scalar.copy, grouped, x_raw[LAST, 0][0], HALF, CHUNK)
+        quantise(LAST, grouped, 0)
+        grouped = interleaved(LAST, 1, "grouped_last")
+        interleave(nc.scalar.copy, grouped, x_raw[LAST, 1][0], 0, CHUNK)
+        quantise(LAST, grouped, 1)
+        place(1, LAST - KEPT_BACK, 1, f"raw_{LAST}_0")
+        place(0, LAST - 1, 2, f"raw_{LAST}_1", CHUNK)
         nc.sync.dma_start(out=out[0:P, :], in_=windows[0][:])
-        place(1, woven, KEPT_BACK, f"grouped_{last}_1")
+        place(1, CHUNKS - KEPT_BACK, KEPT_BACK, "grouped_last")
         nc.sync.dma_start(out=out[P:M, :], in_=windows[1][:])

@@ -211,4 +211,5 @@ def tile_list_hscat_gelu_kernel(tc, x, w, b, wgo, offs, out):
         place(0, LAST - 1, 2, f"raw_{LAST}_1", CHUNK)
         nc.sync.dma_start(out=out[0:P, :], in_=windows[0][:])
         place(1, CHUNKS - KEPT_BACK, KEPT_BACK, "grouped_last")
-        nc.sync.dma_start(out=out[P:M, :], in_=windows[1][:])
+        nc.sync.dma_start(out=out[P:M, 0 : T // 2], in_=windows[1][:, 0 : T // 2])
+        nc.scalar.dma_start(out=out[P:M, T // 2 : T], in_=windows[1][:, T // 2 : T])

@@ -30,7 +30,7 @@ LAST = CHUNKS - 1
 KEPT_BACK = 3
 AHEAD_FROM = 3
 
-VECTOR_COLUMNS = (128, 160)
+VECTOR_COLUMNS = 96
 FACTOR_LOADS = {
     (1, 0): (0, 256),
     (1, 1): (256, 512),
@@ -65,14 +65,15 @@ def tile_list_hscat_gelu_kernel(tc, x, w, b, wgo, offs, out):
         table_loaded = keep.tile([P, 1], F32, name="table_loaded")
         nc.scalar.activation(out=table_loaded[:], in_=zero[:], func=GELU)
 
-        w_raw = []
-        for a in range(PASSES):
-            rows = keep.tile([P, PACK, M], F32, name=f"w_raw_{a}")
+        w_raw = [keep.tile([P, PACK, M], F32, name=f"w_raw_{a}") for a in range(PASSES)]
+
+        def load_w(a):
             nc.sync.dma_start(
-                out=rows[:].rearrange("p i n -> p (i n)"),
+                out=w_raw[a][:].rearrange("p i n -> p (i n)"),
                 in_=w[a * K_PASS : (a + 1) * K_PASS, :].rearrange("(p i) n -> p (i n)", i=PACK),
             )
-            w_raw.append(rows)
+
+        load_w(0)
         x_raw = {}
         factor = keep.tile([P, S], F32, name="factor")
         for c in range(CHUNKS):
@@ -88,6 +89,8 @@ def tile_list_hscat_gelu_kernel(tc, x, w, b, wgo, offs, out):
                         in_=x[a * K_PASS : (a + 1) * K_PASS, j0 : j0 + width].rearrange("(p i) c -> p i c", i=PACK),
                     )
                     x_raw[c, a].append(rows)
+                if (c, a) == (0, 1):
+                    load_w(1)
                 if (c, a) in FACTOR_LOADS:
                     f0, f1 = FACTOR_LOADS[c, a]
                     if f0 == 0:
@@ -101,14 +104,17 @@ def tile_list_hscat_gelu_kernel(tc, x, w, b, wgo, offs, out):
 
         w_codes = keep.tile([P, PASSES * M], U32, name="w_codes", align_bytes=64)
         w_scales = keep.tile([P, PASSES * M], U8, name="w_scales", align_bytes=64)
-        for a in range(PASSES):
-            w_grouped = keep.tile([P, M, PACK], BF16, name=f"w_grouped_{a}", align_bytes=64)
-            interleave(nc.scalar.copy, w_grouped, w_raw[a], 0, M)
+        w_grouped = [keep.tile([P, M, PACK], BF16, name=f"w_grouped_{a}", align_bytes=64) for a in range(PASSES)]
+
+        def quantise_w(a, n0, n1):
             nc.vector.quantize_mx(
-                out=w_codes[:, a * M : (a + 1) * M].bitcast(FP8X4),
-                scales=w_scales[:, a * M : (a + 1) * M],
-                in_=w_grouped[:].rearrange("p n i -> p (n i)"),
+                out=w_codes[:, a * M + n0 : a * M + n1].bitcast(FP8X4),
+                scales=w_scales[:, a * M + n0 : a * M + n1],
+                in_=w_grouped[a][:, n0:n1, :].rearrange("p n i -> p (n i)"),
             )
+
+        interleave(nc.scalar.copy, w_grouped[0], w_raw[0], 0, M)
+        quantise_w(0, 0, M)
 
         x_codes = [keep.tile([P, PASSES * CHUNK], U32, name=f"x_codes_{c}", align_bytes=64) for c in range(CHUNKS)]
         x_scales = [keep.tile([P, PASSES * CHUNK], U8, name=f"x_scales_{c}", align_bytes=64) for c in range(CHUNKS)]
@@ -161,14 +167,21 @@ def tile_list_hscat_gelu_kernel(tc, x, w, b, wgo, offs, out):
             )
 
 
-        for a in range(PASSES):
-            grouped = interleaved(0, 1, f"grouped_0_{a}")
-            interleave(nc.vector.tensor_copy, grouped, x_raw[0, a][0], 0, VECTOR_COLUMNS[a])
-            interleave(nc.scalar.copy, grouped, x_raw[0, a][0], VECTOR_COLUMNS[a], CHUNK)
-            quantise(0, grouped, a)
-        place(0, 0, 1, "results_0_0")
+        grouped = interleaved(0, 1, "grouped_0_0")
+        interleave(nc.scalar.copy, grouped, x_raw[0, 0][0], 0, CHUNK)
+        quantise(0, grouped, 0)
+        grouped = interleaved(0, 1, "grouped_0_1")
+        interleave(nc.vector.tensor_copy, grouped, x_raw[0, 1][0], 0, VECTOR_COLUMNS)
+        interleave(nc.scalar.copy, grouped, x_raw[0, 1][0], VECTOR_COLUMNS, CHUNK)
+        quantise(0, grouped, 1)
+        interleave(nc.vector.tensor_copy, w_grouped[1], w_raw[1], 0, P // 2)
+        interleave(nc.scalar.copy, w_grouped[1], w_raw[1], P // 2, P)
+        quantise_w(1, 0, P)
+        interleave(nc.scalar.copy, w_grouped[1], w_raw[1], P, M)
+        quantise_w(1, P, M)
         grouped = interleaved(1, 1, "grouped_1_0")
         interleave(nc.vector.tensor_copy, grouped, x_raw[1, 0][0], 0, CHUNK)
+        place(0, 0, 1, "results_0_0")
         quantise(1, grouped, 0)
         grouped = interleaved(1, 1, "first_bias")
         for h in range(2):

@@ -178,9 +178,9 @@ def tile_list_hscat_gelu_kernel(tc, x, w, b, wgo, offs, out):
         interleave(nc.scalar.copy, w_grouped[1], w_raw[1], P // 2, P)
         quantise_w(1, 0, P)
         interleave(nc.scalar.copy, w_grouped[1], w_raw[1], P, M)
-        quantise_w(1, P, M)
         grouped = interleaved(1, 1, "grouped_1_0")
         interleave(nc.vector.tensor_copy, grouped, x_raw[1, 0][0], 0, CHUNK)
+        quantise_w(1, P, M)
         place(0, 0, 1, "results_0_0")
         quantise(1, grouped, 0)
         grouped = interleaved(1, 1, "first_bias")

from contextlib import ExitStack

import concourse.mybir as mybir

K, M, T, S = 1024, 256, 4096, 2048
FLOPS = 2 * K * M * S

F32 = mybir.dt.float32
BF16 = mybir.dt.bfloat16
U32 = mybir.dt.uint32
U16 = mybir.dt.uint16
U8 = mybir.dt.uint8
FP8X4 = mybir.dt.float8_e4m3fn_x4
GELU = mybir.ActivationFunctionType.Gelu_apprx_tanh
MULT = mybir.AluOpType.mult

P = 128
PACK = 4
K_PASS = P * PACK
PASSES = K // K_PASS
ROW_TILES = M // P
BANK = 512
PSUM_TURNS = 3
LIST_ROWS = 16

CHUNK = 256
HALF = CHUNK // 2
CHUNKS = S // CHUNK
LAST = CHUNKS - 1
KEPT_BACK = 3
AHEAD_FROM = 3

VECTOR_COLUMNS = 96
FACTOR_LOADS = {
    (1, 0): (0, 256),
    (1, 1): (256, 512),
    (3, 1): (512, 768),
    (4, 1): (768, 1024),
    (5, 1): (1024, 1536),
    (7, 1): (1536, 2048),
}


def interleave(copy, grouped, raw, c0, c1):
    copy(
        out=grouped[:, c0:c1, :].rearrange("p (c i) j -> p c j i", i=2),
        in_=raw[:, :, c0:c1].rearrange("p j (c i) -> p c j i", i=2),
    )


def tile_list_hscat_gelu_kernel(tc, x, w, b, wgo, offs, out):
    nc = tc.nc
    with ExitStack() as ctx:
        keep = ctx.enter_context(tc.tile_pool(name="keep", bufs=1))
        psum = ctx.enter_context(tc.psum_pool(name="psum", bufs=PSUM_TURNS))

        offsets = keep.tile([P, S // LIST_ROWS], U16, name="offsets")

        bias = keep.tile([P, ROW_TILES], F32, name="bias")
        with nc.allow_non_contiguous_dma(reason="one bias to a partition"):
            nc.scalar.dma_start(out=bias[:], in_=b.rearrange("(m p) -> p m", p=P))

        zero = keep.tile([P, 1], F32, name="zero")
        nc.gpsimd.memset(zero[:], 0.0)
        table_loaded = keep.tile([P, 1], F32, name="table_loaded")
        nc.scalar.activation(out=table_loaded[:], in_=zero[:], func=GELU)

        w_raw = [keep.tile([P, PACK, M], F32, name=f"w_raw_{a}") for a in range(PASSES)]

        def load_w(a):
            nc.sync.dma_start(
                out=w_raw[a][:].rearrange("p i n -> p (i n)"),
                in_=w[a * K_PASS : (a + 1) * K_PASS, :].rearrange("(p i) n -> p (i n)", i=PACK),
            )

        load_w(0)
        x_raw = {}
        factor = keep.tile([P, S], F32, name="factor")
        for c in range(CHUNKS):
            for a in range(PASSES):
                width = HALF if (c, a) == (1, 1) else CHUNK
                x_raw[c, a] = []
                for c0 in range(0, CHUNK, width):
                    name = f"raw_{c}_{a}" if c0 == 0 else f"raw_{c}_{a}_second"
                    rows = keep.tile([P, PACK, width], F32, name=name, tag=name, align_bytes=64)
                    j0 = c * CHUNK + c0
                    nc.sync.dma_start(
                        out=rows[:],
                        in_=x[a * K_PASS : (a + 1) * K_PASS, j0 : j0 + width].rearrange("(p i) c -> p i c", i=PACK),
                    )
                    x_raw[c, a].append(rows)
                if (c, a) == (0, 1):
                    load_w(1)
                if (c, a) in FACTOR_LOADS:
                    f0, f1 = FACTOR_LOADS[c, a]
                    if f0 == 0:
                        nc.sync.dma_start(out=offsets[:], in_=offs)
                    nc.sync.dma_start(out=factor[:, f0:f1], in_=wgo[:, f0:f1])

        windows = [keep.tile([P, T], F32, name=f"window_{m}") for m in range(ROW_TILES)]
        nc.vector.memset(windows[0][:], 0.0)
        nc.gpsimd.memset(windows[1][:, 0 : T // 2], 0.0)
        nc.vector.memset(windows[1][:, T // 2 : T], 0.0)

        w_codes = keep.tile([P, PASSES * M], U32, name="w_codes", align_bytes=64)
        w_scales = keep.tile([P, PASSES * M], U8, name="w_scales", align_bytes=64)
        w_grouped = [keep.tile([P, M, PACK], BF16, name=f"w_grouped_{a}", align_bytes=64) for a in range(PASSES)]

        def quantise_w(a, n0, n1):
            nc.vector.quantize_mx(
                out=w_codes[:, a * M + n0 : a * M + n1].bitcast(FP8X4),
                scales=w_scales[:, a * M + n0 : a * M + n1],
                in_=w_grouped[a][:, n0:n1, :].rearrange("p n i -> p (n i)"),
            )

        interleave(nc.scalar.copy, w_grouped[0], w_raw[0], 0, M)
        quantise_w(0, 0, M)

        x_codes = [keep.tile([P, PASSES * CHUNK], U32, name=f"x_codes_{c}", align_bytes=64) for c in range(CHUNKS)]
        x_scales = [keep.tile([P, PASSES * CHUNK], U8, name=f"x_scales_{c}", align_bytes=64) for c in range(CHUNKS)]

        first_bias = keep.tile([P, 1], F32, name="first_bias", tag="first_bias", align_bytes=64)
        nc.scalar.copy(out=first_bias[:], in_=bias[:, 0:1])

        def interleaved(c, passes, slot):
            return keep.tile([P, passes * CHUNK, PACK], BF16, name=f"grouped_{c}_{slot}", tag=slot, align_bytes=64)

        def copy_pass(copy, grouped, c, a, c0=0, c1=CHUNK):
            interleave(copy, grouped[:, a * CHUNK : (a + 1) * CHUNK, :], x_raw[c, a][0], c0, c1)

        def quantise(c, grouped, first_pass=0):
            cols = slice(first_pass * CHUNK, first_pass * CHUNK + grouped.shape[1])
            nc.vector.quantize_mx(
                out=x_codes[c][:, cols].bitcast(FP8X4),
                scales=x_scales[c][:, cols],
                in_=grouped[:].rearrange("p c i -> p (c i)"),
            )

        def place(m, first, count, slot, step=BANK):
            width = count * CHUNK
            results = keep.tile([P, width], F32, name=f"results_{m}_{first}", tag=slot, align_bytes=64)
            row_bias = first_bias[:] if (m, first) == (0, 0) else bias[:, m : m + 1]
            for b0 in range(0, width, step):
                run = min(step, width - b0)
                sums = psum.tile([P, BANK], F32, name=f"sums_{m}_{first}_{b0}", tag=f"sums_{m}")
                for c0 in range(0, run, CHUNK):
                    c = first + (b0 + c0) // CHUNK
                    for a in range(PASSES):
                        x_cols = slice(a * CHUNK, (a + 1) * CHUNK)
                        w_cols = slice(a * M + m * P, a * M + (m + 1) * P)
                        nc.tensor.matmul_mx(
                            out=sums[:, c0 : c0 + CHUNK],
                            lhsT=w_codes[:, w_cols].bitcast(FP8X4),
                            lhsT_scale=w_scales[:, w_cols],
                            rhs=x_codes[c][:, x_cols].bitcast(FP8X4),
                            rhs_scale=x_scales[c][:, x_cols],
                            start=(a == 0),
                            stop=(a == PASSES - 1),
                        )
                nc.scalar.activation(out=results[:, b0 : b0 + run], in_=sums[:, 0:run], func=GELU, bias=row_bias)
            j0 = first * CHUNK
            nc.vector.tensor_tensor(
                windows[m][:].indirect(offsets[:, j0 // LIST_ROWS : (j0 + width) // LIST_ROWS]),
                results[:],
                factor[:, j0 : j0 + width],
                MULT,
            )


        grouped = interleaved(0, 1, "grouped_0_0")
        interleave(nc.scalar.copy, grouped, x_raw[0, 0][0], 0, CHUNK)
        quantise(0, grouped, 0)
        grouped = interleaved(0, 1, "grouped_0_1")
        interleave(nc.vector.tensor_copy, grouped, x_raw[0, 1][0], 0, VECTOR_COLUMNS)
        interleave(nc.scalar.copy, grouped, x_raw[0, 1][0], VECTOR_COLUMNS, CHUNK)
        quantise(0, grouped, 1)
        interleave(nc.vector.tensor_copy, w_grouped[1], w_raw[1], 0, P // 2)
        interleave(nc.scalar.copy, w_grouped[1], w_raw[1], P // 2, P)
        quantise_w(1, 0, P)
        interleave(nc.scalar.copy, w_grouped[1], w_raw[1], P, M)
        grouped = interleaved(1, 1, "grouped_1_0")
        interleave(nc.vector.tensor_copy, grouped, x_raw[1, 0][0], 0, CHUNK)
        quantise_w(1, P, M)
        place(0, 0, 1, "results_0_0")
        quantise(1, grouped, 0)
        grouped = interleaved(1, 1, "first_bias")
        for h in range(2):
            interleave(nc.scalar.copy, grouped[:, h * HALF : (h + 1) * HALF, :], x_raw[1, 1][h], 0, HALF)
        quantise(1, grouped, 1)
        place(1, 0, 1, "raw_1_1")
        place(0, 1, 1, "results_0_1")

        grouped = interleaved(2, 1, "grouped_2_0")
        interleave(nc.scalar.copy, grouped, x_raw[2, 0][0], 0, HALF)
        interleave(nc.scalar.copy, grouped, x_raw[2, 0][0], HALF, CHUNK)
        quantise(2, grouped, 0)
        grouped = interleaved(2, 1, "grouped_2_1")
        interleave(nc.scalar.copy, grouped, x_raw[2, 1][0], 0, CHUNK)
        quantise(2, grouped, 1)
        place(1, 1, 1, "raw_2_0")
        place(0, 2, 1, "results_0_2")

        for c in range(AHEAD_FROM, LAST):
            grouped = interleaved(c, PASSES, f"grouped_{c}")
            copy_pass(nc.scalar.copy, grouped, c, 0)
            if c == AHEAD_FROM + 2:
                place(1, AHEAD_FROM, 1, f"raw_{c - 1}_1")
            copy_pass(nc.scalar.copy, grouped, c, 1)
            quantise(c, grouped)
            if c == AHEAD_FROM:
                place(1, c - 1, 1, f"raw_{c}_0")
            elif c < LAST - 1:
                place(0, c - 1, 1, f"raw_{c}_0")

        grouped = interleaved(LAST, 1, "grouped_last_0")
        interleave(nc.scalar.copy, grouped, x_raw[LAST, 0][0], 0, HALF)
        place(0, LAST - 2, 1, f"raw_{LAST - 1}_1")
        interleave(nc.scalar.copy, grouped, x_raw[LAST, 0][0], HALF, CHUNK)
        quantise(LAST, grouped, 0)
        grouped = interleaved(LAST, 1, "grouped_last")
        interleave(nc.scalar.copy, grouped, x_raw[LAST, 1][0], 0, CHUNK)
        quantise(LAST, grouped, 1)
        place(1, LAST - KEPT_BACK, 1, f"raw_{LAST}_0")
        place(0, LAST - 1, 2, f"raw_{LAST}_1", CHUNK)
        nc.sync.dma_start(out=out[0:P, :], in_=windows[0][:])
        place(1, CHUNKS - KEPT_BACK, KEPT_BACK, "grouped_last")
        nc.sync.dma_start(out=out[P:M, 0 : T // 2], in_=windows[1][:, 0 : T // 2])
        nc.scalar.dma_start(out=out[P:M, T // 2 : T], in_=windows[1][:, T // 2 : T])
